import numpy as np
import ml_dtypes


def mxq(x, axis, fmt="e4m3"):
    dtype, down = {"e4m3": (ml_dtypes.float8_e4m3fn, 7), "e5m2": (ml_dtypes.float8_e5m2, 14)}[fmt]
    v = np.moveaxis(np.asarray(x, np.float32).astype(ml_dtypes.bfloat16).astype(np.float64), axis, -1)
    blocks = v.reshape(v.shape[:-1] + (-1, 32))
    amax = np.abs(blocks).max(-1, keepdims=True)
    byte = np.maximum(np.where(amax > 0, np.frexp(amax)[1] - 1 + 127, 0) - down, 1)
    scale = np.exp2(byte - 127.0)
    codes = (blocks / scale).astype(np.float32).astype(dtype).astype(np.float64)
    return np.moveaxis((codes * scale).reshape(v.shape), -1, axis)


WIDE = False


def mx_kscale(k):
    if not WIDE:
        return np.ones(k)
    levels = np.array([10, -10, 5, -5, 0])
    if k % 512:
        return np.exp2(np.random.permutation(np.resize(levels, k // 32))).repeat(32)
    a = np.empty((k // 512, 16))
    for p in range(k // 512):
        a[p, :8] = np.random.permutation(np.resize(levels, 8))
        for g in range(8):
            far = levels[np.abs(levels - a[p, g]) >= 10]
            a[p, g + 8] = far[np.random.randint(len(far))]
    return np.exp2(a.ravel()).repeat(32)


def f64(x):
    return np.asarray(x).astype(np.float64)


def striped(idx):
    return np.tile(idx.reshape(-1, 16).T, (8, 1)).astype(np.uint16)


def unstriped(offs):
    return offs[:16].T.reshape(-1).astype(np.int64)


def pack_weight(w):
    k, n = w.shape
    w = f64(np.asarray(w, np.float32).astype(ml_dtypes.bfloat16)).reshape(k // 32, 32, n)
    amax = np.abs(w).max(1)
    byte = np.clip(np.where(amax > 0, np.frexp(amax)[1] - 1 + 127 - 7, 1), 1, 254)
    scaled = (w * np.exp2(127.0 - byte)[:, None, :]).reshape(k, n).astype(np.float32)
    words = np.ascontiguousarray(scaled.reshape(k // 512, 128, 4, n).transpose(0, 1, 3, 2)).astype(ml_dtypes.float8_e4m3fn).view(np.uint8)
    return words, np.ascontiguousarray(byte.astype(np.uint8).reshape(k // 512, 16, n))


def unpack_weight(words, scales):
    g, p, n, _ = words.shape
    vals = np.ascontiguousarray(words).view(ml_dtypes.float8_e4m3fn).astype(np.float64) * np.repeat(np.exp2(scales.astype(np.float64) - 127.0), 8, axis=1)[..., None]
    return vals.transpose(0, 1, 3, 2).reshape(g * 512, n)


def gelu(v):
    return 0.5 * v * (1.0 + np.tanh(np.sqrt(2.0 / np.pi) * (v + 0.044715 * v**3)))


K, T, E, C, N = 1536, 512, 4, 256, 128


def by_expert(wq, xq):
    return np.concatenate([wq[e].T @ xq[:, e * C:(e + 1) * C] for e in range(E)], axis=1)


def setup_inputs():
    n = np.random.standard_normal
    s = mx_kscale(K)[:, None]
    first = np.random.permutation(np.repeat(np.arange(E), T // E))
    second = (first + 1 + np.random.permutation(np.repeat(np.arange(E - 1), -(-T // (E - 1)))[:T])) % E
    while np.bincount(second, minlength=E).max() != T // E:
        load = np.bincount(second, minlength=E); hi, lo = int(load.argmax()), int(load.argmin())
        t = np.flatnonzero((second == hi) & (first != lo))[0]; second[t] = lo
    slot_token = np.empty(E * C, np.int64); pos = np.empty((2, T), np.int64); fill = np.zeros(E, np.int64)
    place = np.stack([np.random.permutation(C) for _ in range(E)])
    for r, deal in enumerate((first, second)):
        for t in np.random.permutation(T):
            e = deal[t]; j = e * C + place[e, fill[e]]; fill[e] += 1; slot_token[j] = t; pos[r, t] = j
    g = np.random.uniform(0.2, 0.8, T)
    packed = [pack_weight(m) for m in n((E, K, N)) / np.sqrt(K) / s[None]]
    return {
        "xT": (n((K, T)) * s).astype(np.float32),
        "w_words": np.stack([m[0] for m in packed]),
        "w_scales": np.stack([m[1] for m in packed]),
        "b": (0.3 * n((N, E))).astype(np.float32),
        "gate": np.stack([np.tile(g, (N, 1)), np.tile(1.0 - g, (N, 1))]).astype(np.float32),
        "offs": striped(slot_token),
        "pos1": striped(pos[0]),
        "pos2": striped(pos[1]),
    }


def reference(xT, w_words, w_scales, b, gate, offs, pos1, pos2):
    idx = unstriped(offs)
    xq = mxq(f64(xT)[:, idx], 0, "e4m3")
    w = np.stack([unpack_weight(w_words[e], w_scales[e]) for e in range(E)])
    y = by_expert(w, xq)
    y = gelu(y + np.repeat(f64(b), C, axis=1))
    return f64(gate[0]) * y[:, unstriped(pos1)] + f64(gate[1]) * y[:, unstriped(pos2)]

@@ -1,0 +1,134 @@
+from contextlib import ExitStack
+
+import concourse.mybir as mybir
+
+K, T, E, C, N = 1536, 512, 4, 256, 128
+S = E * C
+FLOPS = 2 * K * N * S
+
+F32 = mybir.dt.float32
+BF16 = mybir.dt.bfloat16
+I32 = mybir.dt.int32
+U32 = mybir.dt.uint32
+U16 = mybir.dt.uint16
+U8 = mybir.dt.uint8
+FP8X4 = mybir.dt.float8_e4m3fn_x4
+GELU = mybir.ActivationFunctionType.Gelu_apprx_tanh
+MULT = mybir.AluOpType.mult
+ADD = mybir.AluOpType.add
+
+P = 128
+PASSES = K // 512
+HALF = T // 2
+VECTOR_TOKENS = 168
+WINDOW = 1376
+
+
+def tile_routed_moe_kernel(tc, xT, w_words, w_scales, b, gate, offs, pos1, pos2, out):
+    nc = tc.nc
+
+    with ExitStack() as ctx:
+        keep = ctx.enter_context(tc.tile_pool(name="keep", bufs=1))
+        psum = ctx.enter_context(tc.psum_pool(name="psum", bufs=1))
+
+        offs_sb = keep.tile([P, S // 16], U16, name="offs_sb")
+        pos1_sb = keep.tile([P, T // 16], U16, name="pos1_sb")
+        pos2_sb = keep.tile([P, T // 16], U16, name="pos2_sb")
+        raw = [[keep.tile([P, 4, HALF], F32, name=f"raw{a}_{h}") for h in range(2)] for a in range(PASSES)]
+        grouped = [keep.tile([P, T, 4], BF16, name=f"grouped{a}", align_bytes=64) for a in range(PASSES)]
+        x_words = [keep.tile([P, WINDOW], I32, name=f"x_words{a}", align_bytes=64) for a in range(PASSES)]
+        x_scales = keep.tile([P, WINDOW], U8, name="x_scales", align_bytes=64)
+        s_words = [keep.tile([P, S], U32, name=f"s_words{a}", align_bytes=64) for a in range(PASSES)]
+        s_scales = keep.tile([P, S], U8, name="s_scales", align_bytes=64)
+        w_sb = keep.tile([P, E * PASSES, N * 4], U8, name="w_sb", align_bytes=64)
+        ws_sb = keep.tile([P, E * PASSES * N], U8, name="ws_sb", align_bytes=64)
+        bias = keep.tile([P, E], F32, name="bias")
+        gate_sb = keep.tile([P, 2, T], F32, name="gate_sb")
+        y = keep.tile([P, S], F32, name="y")
+        t1 = keep.tile([P, T], F32, name="t1")
+        t2 = keep.tile([P, T], F32, name="t2")
+        res = keep.tile([P, T], F32, name="res")
+        warm_in = keep.tile([P, 1], F32, name="warm_in")
+        warm_out = keep.tile([P, 1], F32, name="warm_out")
+        acc = [psum.tile([P, 512], F32, name=f"acc{e}") for e in range(E)]
+
+        nc.vector.memset(warm_in[:], 0.0)
+        nc.scalar.activation(warm_out[:], warm_in[:], GELU)
+        for a in range(PASSES):
+            nc.vector.memset(x_words[a][:, T:WINDOW], 0)
+        nc.gpsimd.memset(x_scales[:], 0)
+        nc.gpsimd.memset(ws_sb[:].bitcast(I32), 0)
+
+        for a in range(PASSES):
+            for h in range(2):
+                nc.sync.dma_start(
+                    out=raw[a][h][:],
+                    in_=xT[512 * a : 512 * (a + 1), h * HALF : (h + 1) * HALF].rearrange("(p j) w -> p j w", j=4),
+                )
+            if a == 0:
+                nc.sync.dma_start(offs_sb[:], offs)
+        ws_view = w_scales.rearrange("e a q n -> q (e a) n")
+        for q in range(4):
+            nc.sync.dma_start(
+                out=ws_sb[32 * q : 32 * q + 4, :].bitcast(I32).rearrange("p (g n) -> p g n", g=E * PASSES),
+                in_=ws_view[4 * q : 4 * q + 4].bitcast(I32),
+            )
+        nc.sync.dma_start(out=w_sb[:], in_=w_words.rearrange("e a p n r -> p (e a) (n r)"))
+        nc.sync.dma_start(bias[:], b)
+        nc.sync.dma_start(pos1_sb[:], pos1)
+        nc.sync.dma_start(pos2_sb[:], pos2)
+        nc.sync.dma_start(out=gate_sb[:], in_=gate.rearrange("r n t -> n r t"))
+
+        def cast(copy, a, h, lo, hi):
+            dst = grouped[a][:, h * HALF + lo : h * HALF + hi, :]
+            copy(out=dst.rearrange("p (c i) t -> p c t i", i=4), in_=raw[a][h][:, :, lo:hi].rearrange("p t (c i) -> p c t i", i=4))
+
+        def quantize(a, lo, hi):
+            nc.vector.quantize_mx(
+                out=x_words[a][:, lo:hi].bitcast(FP8X4),
+                scales=x_scales[4 * a : P, lo:hi],
+                in_=grouped[a][:, lo:hi, :].rearrange("p w t -> p (w t)"),
+            )
+
+        def gather(dst, src, lo, hi):
+            nc.vector.tensor_copy(dst[:, lo:hi], src.indirect(offs_sb[:, lo // 16 : hi // 16]))
+
+        def multiply(a, e):
+            g = PASSES * e + a
+            cols = slice(e * C, (e + 1) * C)
+            nc.tensor.matmul_mx(
+                out=acc[e][:, 0:C],
+                lhsT=w_sb[:, g, :].bitcast(FP8X4),
+                lhsT_scale=ws_sb[:, g * N : (g + 1) * N],
+                rhs=s_words[a][:, cols].bitcast(FP8X4),
+                rhs_scale=s_scales[4 * a : P, cols],
+                start=(a == 0),
+                stop=(a == PASSES - 1),
+            )
+
+        for h in range(2):
+            cast(nc.vector.tensor_copy, 0, h, 0, VECTOR_TOKENS)
+            cast(nc.scalar.copy, 0, h, VECTOR_TOKENS, HALF)
+            quantize(0, h * HALF, (h + 1) * HALF)
+        for a in range(1, PASSES):
+            for h in range(2):
+                cast(nc.scalar.copy, a, h, 0, HALF)
+        gather(s_words[0], x_words[0][:].bitcast(U32), 0, S)
+        quantize(1, 0, T)
+        gather(s_words[1], x_words[1][:].bitcast(U32), 0, S)
+        quantize(2, 0, T)
+        gather(s_scales, x_scales[:], 0, S)
+        for a in range(2):
+            for e in range(E):
+                multiply(a, e)
+        gather(s_words[2], x_words[2][:].bitcast(U32), 0, S - C)
+        gather(s_words[2], x_words[2][:].bitcast(U32), S - C, S)
+        for e in range(E):
+            multiply(2, e)
+            nc.scalar.activation(y[:, e * C : (e + 1) * C], acc[e][:, 0:C], GELU, bias=bias[:, e : e + 1])
+        nc.vector.tensor_tensor(t1[:], y[:].indirect(pos1_sb[:]), gate_sb[:, 0, :], MULT)
+        nc.vector.tensor_tensor(t2[:], y[:].indirect(pos2_sb[:]), gate_sb[:, 1, :], MULT)
+        for h in range(2):
+            cols = slice(h * HALF, (h + 1) * HALF)
+            nc.vector.tensor_tensor(res[:, cols], t1[:, cols], t2[:, cols], ADD)
+            nc.sync.dma_start(out=out[:, cols], in_=res[:, cols])

@@ -22,6 +22,8 @@ PASSES = K // 512
 HALF = T // 2
 VECTOR_TOKENS = 168
 WINDOW = 1376
+LAST_CUTS = ((0, 384), (384, 768), (768, 896), (896, 1024))
+GROUPS = ((0, 0, 256), (1, 256, 512), (2, 512, 768), (3, 768, 896), (3, 896, 1024))
 
 
 def tile_routed_moe_kernel(tc, xT, w_words, w_scales, b, gate, offs, pos1, pos2, out):
@@ -36,7 +38,7 @@ def tile_routed_moe_kernel(tc, xT, w_words, w_scales, b, gate, offs, pos1, pos2,
         pos2_sb = keep.tile([P, T // 16], U16, name="pos2_sb")
         raw = [[keep.tile([P, 4, HALF], F32, name=f"raw{a}_{h}") for h in range(2)] for a in range(PASSES)]
         grouped = [keep.tile([P, T, 4], BF16, name=f"grouped{a}", align_bytes=64) for a in range(PASSES)]
-        x_words = [keep.tile([P, WINDOW], I32, name=f"x_words{a}", align_bytes=64) for a in range(PASSES)]
+        x_words = [keep.tile([P, WINDOW if a < 2 else T], I32, name=f"x_words{a}", align_bytes=64) for a in range(PASSES)]
         x_scales = keep.tile([P, WINDOW], U8, name="x_scales", align_bytes=64)
         s_words = [keep.tile([P, S], U32, name=f"s_words{a}", align_bytes=64) for a in range(PASSES)]
         s_scales = keep.tile([P, S], U8, name="s_scales", align_bytes=64)
@@ -50,11 +52,11 @@ def tile_routed_moe_kernel(tc, xT, w_words, w_scales, b, gate, offs, pos1, pos2,
         res = keep.tile([P, T], F32, name="res")
         warm_in = keep.tile([P, 1], F32, name="warm_in")
         warm_out = keep.tile([P, 1], F32, name="warm_out")
-        acc = [psum.tile([P, 512], F32, name=f"acc{e}") for e in range(E)]
+        acc = [psum.tile([P, 512], F32, name=f"acc{i}") for i in range(len(GROUPS))]
 
         nc.vector.memset(warm_in[:], 0.0)
         nc.scalar.activation(warm_out[:], warm_in[:], GELU)
-        for a in range(PASSES):
+        for a in range(2):
             nc.vector.memset(x_words[a][:, T:WINDOW], 0)
         nc.gpsimd.memset(x_scales[:], 0)
         nc.gpsimd.memset(ws_sb[:].bitcast(I32), 0)
@@ -93,15 +95,15 @@ def tile_routed_moe_kernel(tc, xT, w_words, w_scales, b, gate, offs, pos1, pos2,
         def gather(dst, src, lo, hi):
             nc.vector.tensor_copy(dst[:, lo:hi], src.indirect(offs_sb[:, lo // 16 : hi // 16]))
 
-        def multiply(a, e):
+        def multiply(a, i):
+            e, lo, hi = GROUPS[i]
             g = PASSES * e + a
-            cols = slice(e * C, (e + 1) * C)
             nc.tensor.matmul_mx(
-                out=acc[e][:, 0:C],
+                out=acc[i][:, 0 : hi - lo],
                 lhsT=w_sb[:, g, :].bitcast(FP8X4),
                 lhsT_scale=ws_sb[:, g * N : (g + 1) * N],
-                rhs=s_words[a][:, cols].bitcast(FP8X4),
-                rhs_scale=s_scales[4 * a : P, cols],
+                rhs=s_words[a][:, lo:hi].bitcast(FP8X4),
+                rhs_scale=s_scales[4 * a : P, lo:hi],
                 start=(a == 0),
                 stop=(a == PASSES - 1),
             )
@@ -110,24 +112,29 @@ def tile_routed_moe_kernel(tc, xT, w_words, w_scales, b, gate, offs, pos1, pos2,
             cast(nc.vector.tensor_copy, 0, h, 0, VECTOR_TOKENS)
             cast(nc.scalar.copy, 0, h, VECTOR_TOKENS, HALF)
             quantize(0, h * HALF, (h + 1) * HALF)
-        for a in range(1, PASSES):
-            for h in range(2):
-                cast(nc.scalar.copy, a, h, 0, HALF)
+        cast(nc.scalar.copy, 1, 0, 0, HALF)
+        cast(nc.scalar.copy, 1, 1, 0, 192)
+        cast(nc.vector.tensor_copy, 1, 1, 192, HALF)
+        for h in range(2):
+            cast(nc.scalar.copy, 2, h, 0, HALF)
         gather(s_words[0], x_words[0][:].bitcast(U32), 0, S)
         quantize(1, 0, T)
         gather(s_words[1], x_words[1][:].bitcast(U32), 0, S)
         quantize(2, 0, T)
         gather(s_scales, x_scales[:], 0, S)
         for a in range(2):
-            for e in range(E):
-                multiply(a, e)
-        gather(s_words[2], x_words[2][:].bitcast(U32), 0, S - C)
-        gather(s_words[2], x_words[2][:].bitcast(U32), S - C, S)
-        for e in range(E):
-            multiply(2, e)
-            nc.scalar.activation(y[:, e * C : (e + 1) * C], acc[e][:, 0:C], GELU, bias=bias[:, e : e + 1])
+            for i in range(len(GROUPS)):
+                multiply(a, i)
+        for lo, hi in LAST_CUTS:
+            gather(s_words[2], x_words[2][:].bitcast(U32), lo, hi)
+        for i, (e, lo, hi) in enumerate(GROUPS):
+            multiply(2, i)
+            nc.scalar.activation(y[:, lo:hi], acc[i][:, 0 : hi - lo], GELU, bias=bias[:, e : e + 1])
         nc.vector.tensor_tensor(t1[:], y[:].indirect(pos1_sb[:]), gate_sb[:, 0, :], MULT)
-        nc.vector.tensor_tensor(t2[:], y[:].indirect(pos2_sb[:]), gate_sb[:, 1, :], MULT)
+        for h in range(2):
+            cols = slice(h * HALF, (h + 1) * HALF)
+            lists = slice(h * HALF // 16, (h + 1) * HALF // 16)
+            nc.vector.tensor_tensor(t2[:, cols], y[:].indirect(pos2_sb[:, lists]), gate_sb[:, 1, cols], MULT)
         for h in range(2):
             cols = slice(h * HALF, (h + 1) * HALF)
             nc.vector.tensor_tensor(res[:, cols], t1[:, cols], t2[:, cols], ADD)

@@ -20,9 +20,13 @@ ADD = mybir.AluOpType.add
 P = 128
 PASSES = K // 512
 HALF = T // 2
-VECTOR_TOKENS = 168
 WINDOW = 1376
-LAST_CUTS = ((0, 384), (384, 768), (768, 896), (896, 1024))
+OUT_CUTS = ((0, 384), (384, 512))
+STEPS = (
+    ((0, 384), ((0, 384),), (0,)),
+    ((384, 768), ((384, 768),), (1, 2)),
+    ((768, 1024), ((768, 896), (896, 1024)), (3, 4)),
+)
 GROUPS = ((0, 0, 256), (1, 256, 512), (2, 512, 768), (3, 768, 896), (3, 896, 1024))
 
 
@@ -36,10 +40,10 @@ def tile_routed_moe_kernel(tc, xT, w_words, w_scales, b, gate, offs, pos1, pos2,
         offs_sb = keep.tile([P, S // 16], U16, name="offs_sb")
         pos1_sb = keep.tile([P, T // 16], U16, name="pos1_sb")
         pos2_sb = keep.tile([P, T // 16], U16, name="pos2_sb")
-        raw = [[keep.tile([P, 4, HALF], F32, name=f"raw{a}_{h}") for h in range(2)] for a in range(PASSES)]
+        raw = [keep.tile([P, 4, T], F32, name=f"raw{a}") for a in range(PASSES)]
         grouped = [keep.tile([P, T, 4], BF16, name=f"grouped{a}", align_bytes=64) for a in range(PASSES)]
         x_words = [keep.tile([P, WINDOW if a < 2 else T], I32, name=f"x_words{a}", align_bytes=64) for a in range(PASSES)]
-        x_scales = keep.tile([P, WINDOW], U8, name="x_scales", align_bytes=64)
+        x_scales = keep.tile([P, T], U8, name="x_scales", align_bytes=64)
         s_words = [keep.tile([P, S], U32, name=f"s_words{a}", align_bytes=64) for a in range(PASSES)]
         s_scales = keep.tile([P, S], U8, name="s_scales", align_bytes=64)
         w_sb = keep.tile([P, E * PASSES, N * 4], U8, name="w_sb", align_bytes=64)
@@ -62,11 +66,7 @@ def tile_routed_moe_kernel(tc, xT, w_words, w_scales, b, gate, offs, pos1, pos2,
         nc.gpsimd.memset(ws_sb[:].bitcast(I32), 0)
 
         for a in range(PASSES):
-            for h in range(2):
-                nc.sync.dma_start(
-                    out=raw[a][h][:],
-                    in_=xT[512 * a : 512 * (a + 1), h * HALF : (h + 1) * HALF].rearrange("(p j) w -> p j w", j=4),
-                )
+            nc.sync.dma_start(out=raw[a][:], in_=xT[512 * a : 512 * (a + 1), :].rearrange("(p j) w -> p j w", j=4))
             if a == 0:
                 nc.sync.dma_start(offs_sb[:], offs)
         ws_view = w_scales.rearrange("e a q n -> q (e a) n")
@@ -81,9 +81,9 @@ def tile_routed_moe_kernel(tc, xT, w_words, w_scales, b, gate, offs, pos1, pos2,
         nc.sync.dma_start(pos2_sb[:], pos2)
         nc.sync.dma_start(out=gate_sb[:], in_=gate.rearrange("r n t -> n r t"))
 
-        def cast(copy, a, h, lo, hi):
-            dst = grouped[a][:, h * HALF + lo : h * HALF + hi, :]
-            copy(out=dst.rearrange("p (c i) t -> p c t i", i=4), in_=raw[a][h][:, :, lo:hi].rearrange("p t (c i) -> p c t i", i=4))
+        def cast(copy, a, lo, hi):
+            dst = grouped[a][:, lo:hi, :]
+            copy(out=dst.rearrange("p (c i) t -> p c t i", i=4), in_=raw[a][:, :, lo:hi].rearrange("p t (c i) -> p c t i", i=4))
 
         def quantize(a, lo, hi):
             nc.vector.quantize_mx(
@@ -108,34 +108,31 @@ def tile_routed_moe_kernel(tc, xT, w_words, w_scales, b, gate, offs, pos1, pos2,
                 stop=(a == PASSES - 1),
             )
 
-        for h in range(2):
-            cast(nc.vector.tensor_copy, 0, h, 0, VECTOR_TOKENS)
-            cast(nc.scalar.copy, 0, h, VECTOR_TOKENS, HALF)
-            quantize(0, h * HALF, (h + 1) * HALF)
-        cast(nc.scalar.copy, 1, 0, 0, HALF)
-        cast(nc.scalar.copy, 1, 1, 0, 192)
-        cast(nc.vector.tensor_copy, 1, 1, 192, HALF)
-        for h in range(2):
-            cast(nc.scalar.copy, 2, h, 0, HALF)
+        cast(nc.vector.tensor_copy, 0, 0, 320)
+        cast(nc.scalar.copy, 0, 320, T)
+        quantize(0, 0, HALF)
+        quantize(0, HALF, T)
         gather(s_words[0], x_words[0][:].bitcast(U32), 0, S)
+        cast(nc.scalar.copy, 1, 0, 384)
+        cast(nc.vector.tensor_copy, 1, 384, T)
         quantize(1, 0, T)
         gather(s_words[1], x_words[1][:].bitcast(U32), 0, S)
+        cast(nc.scalar.copy, 2, 0, T)
         quantize(2, 0, T)
-        gather(s_scales, x_scales[:], 0, S)
-        for a in range(2):
-            for i in range(len(GROUPS)):
-                multiply(a, i)
-        for lo, hi in LAST_CUTS:
-            gather(s_words[2], x_words[2][:].bitcast(U32), lo, hi)
-        for i, (e, lo, hi) in enumerate(GROUPS):
-            multiply(2, i)
-            nc.scalar.activation(y[:, lo:hi], acc[i][:, 0 : hi - lo], GELU, bias=bias[:, e : e + 1])
+        for scale_cut, word_cuts, groups in STEPS:
+            gather(s_scales, x_scales[:], *scale_cut)
+            for a in range(2):
+                for i in groups:
+                    multiply(a, i)
+            for lo, hi in word_cuts:
+                gather(s_words[2], x_words[2][:].bitcast(U32), lo, hi)
+            for i in groups:
+                multiply(2, i)
+                e, lo, hi = GROUPS[i]
+                nc.scalar.activation(y[:, lo:hi], acc[i][:, 0 : hi - lo], GELU, bias=bias[:, e : e + 1])
         nc.vector.tensor_tensor(t1[:], y[:].indirect(pos1_sb[:]), gate_sb[:, 0, :], MULT)
-        for h in range(2):
-            cols = slice(h * HALF, (h + 1) * HALF)
-            lists = slice(h * HALF // 16, (h + 1) * HALF // 16)
-            nc.vector.tensor_tensor(t2[:, cols], y[:].indirect(pos2_sb[:, lists]), gate_sb[:, 1, cols], MULT)
-        for h in range(2):
-            cols = slice(h * HALF, (h + 1) * HALF)
-            nc.vector.tensor_tensor(res[:, cols], t1[:, cols], t2[:, cols], ADD)
-            nc.sync.dma_start(out=out[:, cols], in_=res[:, cols])
+        for lo, hi in OUT_CUTS:
+            nc.vector.tensor_tensor(t2[:, lo:hi], y[:].indirect(pos2_sb[:, lo // 16 : hi // 16]), gate_sb[:, 1, lo:hi], MULT)
+        for lo, hi in OUT_CUTS:
+            nc.vector.tensor_tensor(res[:, lo:hi], t1[:, lo:hi], t2[:, lo:hi], ADD)
+            nc.sync.dma_start(out=out[:, lo:hi], in_=res[:, lo:hi])

@@ -20,7 +20,8 @@ ADD = mybir.AluOpType.add
 P = 128
 PASSES = K // 512
 HALF = T // 2
-WINDOW = 1376
+PAIRS = (slice(0, 2), slice(2, 4))
+ALL_ROWS = slice(0, 4)
 OUT_CUTS = ((0, 384), (384, 512))
 STEPS = (
     ((0, 384), ((0, 384),), (0,)),
@@ -42,7 +43,7 @@ def tile_routed_moe_kernel(tc, xT, w_words, w_scales, b, gate, offs, pos1, pos2,
         pos2_sb = keep.tile([P, T // 16], U16, name="pos2_sb")
         raw = [keep.tile([P, 4, T], F32, name=f"raw{a}") for a in range(PASSES)]
         grouped = [keep.tile([P, T, 4], BF16, name=f"grouped{a}", align_bytes=64) for a in range(PASSES)]
-        x_words = [keep.tile([P, WINDOW if a < 2 else T], I32, name=f"x_words{a}", align_bytes=64) for a in range(PASSES)]
+        x_words = [keep.tile([P, T], U32, name=f"x_words{a}", align_bytes=64) for a in range(PASSES)]
         x_scales = keep.tile([P, T], U8, name="x_scales", align_bytes=64)
         s_words = [keep.tile([P, S], U32, name=f"s_words{a}", align_bytes=64) for a in range(PASSES)]
         s_scales = keep.tile([P, S], U8, name="s_scales", align_bytes=64)
@@ -60,15 +61,15 @@ def tile_routed_moe_kernel(tc, xT, w_words, w_scales, b, gate, offs, pos1, pos2,
 
         nc.vector.memset(warm_in[:], 0.0)
         nc.scalar.activation(warm_out[:], warm_in[:], GELU)
-        for a in range(2):
-            nc.vector.memset(x_words[a][:, T:WINDOW], 0)
         nc.gpsimd.memset(x_scales[:], 0)
         nc.gpsimd.memset(ws_sb[:].bitcast(I32), 0)
 
-        for a in range(PASSES):
-            nc.sync.dma_start(out=raw[a][:], in_=xT[512 * a : 512 * (a + 1), :].rearrange("(p j) w -> p j w", j=4))
-            if a == 0:
-                nc.sync.dma_start(offs_sb[:], offs)
+        x_views = [xT[512 * a : 512 * (a + 1), :].rearrange("(p j) w -> p j w", j=4) for a in range(PASSES)]
+        for pair in PAIRS:
+            nc.sync.dma_start(out=raw[0][:, pair, :], in_=x_views[0][:, pair, :])
+        nc.sync.dma_start(offs_sb[:], offs)
+        for a in range(1, PASSES):
+            nc.sync.dma_start(out=raw[a][:], in_=x_views[a])
         ws_view = w_scales.rearrange("e a q n -> q (e a) n")
         for q in range(4):
             nc.sync.dma_start(
@@ -81,9 +82,11 @@ def tile_routed_moe_kernel(tc, xT, w_words, w_scales, b, gate, offs, pos1, pos2,
         nc.sync.dma_start(pos2_sb[:], pos2)
         nc.sync.dma_start(out=gate_sb[:], in_=gate.rearrange("r n t -> n r t"))
 
-        def cast(copy, a, lo, hi):
-            dst = grouped[a][:, lo:hi, :]
-            copy(out=dst.rearrange("p (c i) t -> p c t i", i=4), in_=raw[a][:, :, lo:hi].rearrange("p t (c i) -> p c t i", i=4))
+        def cast(copy, a, lo, hi, rows=ALL_ROWS):
+            copy(
+                out=grouped[a][:, lo:hi, rows].rearrange("p (c i) t -> p c t i", i=4),
+                in_=raw[a][:, rows, lo:hi].rearrange("p t (c i) -> p c t i", i=4),
+            )
 
         def quantize(a, lo, hi):
             nc.vector.quantize_mx(
@@ -108,24 +111,31 @@ def tile_routed_moe_kernel(tc, xT, w_words, w_scales, b, gate, offs, pos1, pos2,
                 stop=(a == PASSES - 1),
             )
 
-        cast(nc.vector.tensor_copy, 0, 0, 320)
-        cast(nc.scalar.copy, 0, 320, T)
+        cast(nc.vector.tensor_copy, 0, 0, 344, PAIRS[0])
+        cast(nc.scalar.copy, 0, 344, T, PAIRS[0])
+        cast(nc.vector.tensor_copy, 0, 0, HALF, PAIRS[1])
+        cast(nc.scalar.copy, 0, 344, T, PAIRS[1])
+        cast(nc.vector.tensor_copy, 0, HALF, 344, PAIRS[1])
         quantize(0, 0, HALF)
         quantize(0, HALF, T)
-        gather(s_words[0], x_words[0][:].bitcast(U32), 0, S)
-        cast(nc.scalar.copy, 1, 0, 384)
-        cast(nc.vector.tensor_copy, 1, 384, T)
+        gather(s_words[0], x_words[0][:], 0, 384)
+        cast(nc.scalar.copy, 1, 0, 304)
+        cast(nc.vector.tensor_copy, 1, 304, T)
+        gather(s_words[0], x_words[0][:], 384, 768)
         quantize(1, 0, T)
-        gather(s_words[1], x_words[1][:].bitcast(U32), 0, S)
+        gather(s_words[0], x_words[0][:], 768, S)
         cast(nc.scalar.copy, 2, 0, T)
+        gather(s_words[1], x_words[1][:], 0, 384)
+        gather(s_words[1], x_words[1][:], 384, 768)
         quantize(2, 0, T)
+        gather(s_words[1], x_words[1][:], 768, S)
         for scale_cut, word_cuts, groups in STEPS:
             gather(s_scales, x_scales[:], *scale_cut)
             for a in range(2):
                 for i in groups:
                     multiply(a, i)
             for lo, hi in word_cuts:
-                gather(s_words[2], x_words[2][:].bitcast(U32), lo, hi)
+                gather(s_words[2], x_words[2][:], lo, hi)
             for i in groups:
                 multiply(2, i)
                 e, lo, hi = GROUPS[i]

from contextlib import ExitStack

import concourse.mybir as mybir

K, T, E, C, N = 1536, 512, 4, 256, 128
S = E * C
FLOPS = 2 * K * N * S

F32 = mybir.dt.float32
BF16 = mybir.dt.bfloat16
I32 = mybir.dt.int32
U32 = mybir.dt.uint32
U16 = mybir.dt.uint16
U8 = mybir.dt.uint8
FP8X4 = mybir.dt.float8_e4m3fn_x4
GELU = mybir.ActivationFunctionType.Gelu_apprx_tanh
MULT = mybir.AluOpType.mult
ADD = mybir.AluOpType.add

P = 128
PASSES = K // 512
HALF = T // 2
PAIRS = (slice(0, 2), slice(2, 4))
ALL_ROWS = slice(0, 4)
OUT_CUTS = ((0, 384), (384, 512))
STEPS = (
    ((0, 384), ((0, 384),), (0,)),
    ((384, 768), ((384, 768),), (1, 2)),
    ((768, 1024), ((768, 896), (896, 1024)), (3, 4)),
)
GROUPS = ((0, 0, 256), (1, 256, 512), (2, 512, 768), (3, 768, 896), (3, 896, 1024))


def tile_routed_moe_kernel(tc, xT, w_words, w_scales, b, gate, offs, pos1, pos2, out):
    nc = tc.nc

    with ExitStack() as ctx:
        keep = ctx.enter_context(tc.tile_pool(name="keep", bufs=1))
        psum = ctx.enter_context(tc.psum_pool(name="psum", bufs=1))

        offs_sb = keep.tile([P, S // 16], U16, name="offs_sb")
        pos1_sb = keep.tile([P, T // 16], U16, name="pos1_sb")
        pos2_sb = keep.tile([P, T // 16], U16, name="pos2_sb")
        raw = [keep.tile([P, 4, T], F32, name=f"raw{a}") for a in range(PASSES)]
        grouped = [keep.tile([P, T, 4], BF16, name=f"grouped{a}", align_bytes=64) for a in range(PASSES)]
        x_words = [keep.tile([P, T], U32, name=f"x_words{a}", align_bytes=64) for a in range(PASSES)]
        x_scales = keep.tile([P, T], U8, name="x_scales", align_bytes=64)
        s_words = [keep.tile([P, S], U32, name=f"s_words{a}", align_bytes=64) for a in range(PASSES)]
        s_scales = keep.tile([P, S], U8, name="s_scales", align_bytes=64)
        w_sb = keep.tile([P, E * PASSES, N * 4], U8, name="w_sb", align_bytes=64)
        ws_sb = keep.tile([P, E * PASSES * N], U8, name="ws_sb", align_bytes=64)
        bias = keep.tile([P, E], F32, name="bias")
        gate_sb = keep.tile([P, 2, T], F32, name="gate_sb")
        y = keep.tile([P, S], F32, name="y")
        t1 = keep.tile([P, T], F32, name="t1")
        t2 = keep.tile([P, T], F32, name="t2")
        res = keep.tile([P, T], F32, name="res")
        warm_in = keep.tile([P, 1], F32, name="warm_in")
        warm_out = keep.tile([P, 1], F32, name="warm_out")
        acc = [psum.tile([P, 512], F32, name=f"acc{i}") for i in range(len(GROUPS))]

        nc.vector.memset(warm_in[:], 0.0)
        nc.scalar.activation(warm_out[:], warm_in[:], GELU)
        nc.gpsimd.memset(x_scales[:], 0)
        nc.gpsimd.memset(ws_sb[:].bitcast(I32), 0)

        x_views = [xT[512 * a : 512 * (a + 1), :].rearrange("(p j) w -> p j w", j=4) for a in range(PASSES)]
        for pair in PAIRS:
            nc.sync.dma_start(out=raw[0][:, pair, :], in_=x_views[0][:, pair, :])
        nc.sync.dma_start(offs_sb[:], offs)
        for a in range(1, PASSES):
            nc.sync.dma_start(out=raw[a][:], in_=x_views[a])
        ws_view = w_scales.rearrange("e a q n -> q (e a) n")
        for q in range(4):
            nc.sync.dma_start(
                out=ws_sb[32 * q : 32 * q + 4, :].bitcast(I32).rearrange("p (g n) -> p g n", g=E * PASSES),
                in_=ws_view[4 * q : 4 * q + 4].bitcast(I32),
            )
        nc.sync.dma_start(out=w_sb[:], in_=w_words.rearrange("e a p n r -> p (e a) (n r)"))
        nc.sync.dma_start(bias[:], b)
        nc.sync.dma_start(pos1_sb[:], pos1)
        nc.sync.dma_start(pos2_sb[:], pos2)
        nc.sync.dma_start(out=gate_sb[:], in_=gate.rearrange("r n t -> n r t"))

        def cast(copy, a, lo, hi, rows=ALL_ROWS):
            copy(
                out=grouped[a][:, lo:hi, rows].rearrange("p (c i) t -> p c t i", i=4),
                in_=raw[a][:, rows, lo:hi].rearrange("p t (c i) -> p c t i", i=4),
            )

        def quantize(a, lo, hi):
            nc.vector.quantize_mx(
                out=x_words[a][:, lo:hi].bitcast(FP8X4),
                scales=x_scales[4 * a : P, lo:hi],
                in_=grouped[a][:, lo:hi, :].rearrange("p w t -> p (w t)"),
            )

        def gather(dst, src, lo, hi):
            nc.vector.tensor_copy(dst[:, lo:hi], src.indirect(offs_sb[:, lo // 16 : hi // 16]))

        def multiply(a, i):
            e, lo, hi = GROUPS[i]
            g = PASSES * e + a
            nc.tensor.matmul_mx(
                out=acc[i][:, 0 : hi - lo],
                lhsT=w_sb[:, g, :].bitcast(FP8X4),
                lhsT_scale=ws_sb[:, g * N : (g + 1) * N],
                rhs=s_words[a][:, lo:hi].bitcast(FP8X4),
                rhs_scale=s_scales[4 * a : P, lo:hi],
                start=(a == 0),
                stop=(a == PASSES - 1),
            )

        cast(nc.vector.tensor_copy, 0, 0, 344, PAIRS[0])
        cast(nc.scalar.copy, 0, 344, T, PAIRS[0])
        cast(nc.vector.tensor_copy, 0, 0, HALF, PAIRS[1])
        cast(nc.scalar.copy, 0, 344, T, PAIRS[1])
        cast(nc.vector.tensor_copy, 0, HALF, 344, PAIRS[1])
        quantize(0, 0, HALF)
        quantize(0, HALF, T)
        gather(s_words[0], x_words[0][:], 0, 384)
        cast(nc.scalar.copy, 1, 0, 304)
        cast(nc.vector.tensor_copy, 1, 304, T)
        gather(s_words[0], x_words[0][:], 384, 768)
        quantize(1, 0, T)
        gather(s_words[0], x_words[0][:], 768, S)
        cast(nc.scalar.copy, 2, 0, T)
        gather(s_words[1], x_words[1][:], 0, 384)
        gather(s_words[1], x_words[1][:], 384, 768)
        quantize(2, 0, T)
        gather(s_words[1], x_words[1][:], 768, S)
        for scale_cut, word_cuts, groups in STEPS:
            gather(s_scales, x_scales[:], *scale_cut)
            for a in range(2):
                for i in groups:
                    multiply(a, i)
            for lo, hi in word_cuts:
                gather(s_words[2], x_words[2][:], lo, hi)
            for i in groups:
                multiply(2, i)
                e, lo, hi = GROUPS[i]
                nc.scalar.activation(y[:, lo:hi], acc[i][:, 0 : hi - lo], GELU, bias=bias[:, e : e + 1])
        nc.vector.tensor_tensor(t1[:], y[:].indirect(pos1_sb[:]), gate_sb[:, 0, :], MULT)
        for lo, hi in OUT_CUTS:
            nc.vector.tensor_tensor(t2[:, lo:hi], y[:].indirect(pos2_sb[:, lo // 16 : hi // 16]), gate_sb[:, 1, lo:hi], MULT)
        for lo, hi in OUT_CUTS:
            nc.vector.tensor_tensor(res[:, lo:hi], t1[:, lo:hi], t2[:, lo:hi], ADD)
            nc.sync.dma_start(out=out[:, lo:hi], in_=res[:, lo:hi])
